import numpy as np
import ml_dtypes

BF16 = ml_dtypes.bfloat16


def bf(x):
    return np.asarray(x, np.float32).astype(BF16)


def f32(x):
    return np.asarray(x, np.float32)


def f64(x):
    return np.asarray(x).astype(np.float64)


def striped(idx):
    return np.concatenate([l.reshape(-1, 16).T for l in idx])


def rows(idx, k):
    return np.tile(np.repeat(idx, 16, axis=0), (k // (16 * 8), 1))


def look(tab, idx):
    return np.take_along_axis(f64(tab), rows(idx, len(tab)), axis=1)


K, S, V, N = 512, 2048, 1024, 1024


def setup_inputs():
    return {"tab": f32(np.random.standard_normal((2, K, S))), "y": f32(np.random.standard_normal((K, V))), "offs": striped(np.stack([np.random.permutation(S)[:N] for _ in range(8)]))}


def reference(tab, y, offs):
    idx = np.stack([g.T.reshape(-1) for g in np.split(offs, 8)])
    x = (look(tab[0], idx) + f64(y)) * (1.0 / (1.0 + np.exp(-look(tab[1], idx))))
    return x

@@ -1,0 +1,55 @@
+import concourse.mybir as mybir
+
+F32, U16 = mybir.dt.float32, mybir.dt.uint16
+ADD, MULT = mybir.AluOpType.add, mybir.AluOpType.mult
+SIGMOID = mybir.ActivationFunctionType.Sigmoid
+
+P = 128
+PIECE = 512
+PER_COLUMN = 16
+
+
+def tile_lookup_vg_addsig_out_kernel(tc, tab, y, offs, out):
+    nc = tc.nc
+    rows, n = y.shape
+    places = tab.shape[2]
+    blocks = rows // P
+    pieces = n // PIECE
+
+    with (
+        tc.tile_pool(name="lists", bufs=1) as lists,
+        tc.tile_pool(name="loads", bufs=blocks) as loads,
+        tc.tile_pool(name="work", bufs=blocks * pieces) as work,
+    ):
+        offsets = lists.tile([P, n // PER_COLUMN], U16, name="offsets")
+        nc.sync.dma_start(offsets[:], offs)
+
+        values, streams, gates = [], [], []
+        for b in range(blocks):
+            block = slice(b * P, (b + 1) * P)
+            value = loads.tile([P, places], F32, name="value")
+            stream = loads.tile([P, n], F32, name="stream")
+            gate = loads.tile([P, places], F32, name="gate")
+            nc.sync.dma_start(value[:], tab[0, block, :])
+            nc.sync.dma_start(stream[:], y[block, :])
+            nc.sync.dma_start(gate[:], tab[1, block, :])
+            values.append(value)
+            streams.append(stream)
+            gates.append(gate)
+
+        for b in range(blocks):
+            block = slice(b * P, (b + 1) * P)
+            sums, opened = [], []
+            for p in range(pieces):
+                piece = slice(p * PIECE, (p + 1) * PIECE)
+                part = offsets[:, p * PIECE // PER_COLUMN : (p + 1) * PIECE // PER_COLUMN]
+                total = work.tile([P, PIECE], F32, name="total")
+                nc.vector.tensor_tensor(total[:], values[b][:].indirect(part), streams[b][:, piece], ADD)
+                sums.append(total)
+                openness = work.tile([P, PIECE], F32, name="openness")
+                nc.scalar.activation(openness[:], gates[b][:].indirect(part), SIGMOID)
+                opened.append(openness)
+            for p in range(pieces):
+                product = work.tile([P, PIECE], F32, name="product")
+                nc.vector.tensor_tensor(product[:], sums[p][:], opened[p][:], MULT)
+                nc.sync.dma_start(out[block, p * PIECE : (p + 1) * PIECE], product[:])

@@ -19,7 +19,7 @@ def tile_lookup_vg_addsig_out_kernel(tc, tab, y, offs, out):
     with (
         tc.tile_pool(name="lists", bufs=1) as lists,
         tc.tile_pool(name="loads", bufs=blocks) as loads,
-        tc.tile_pool(name="work", bufs=blocks * pieces) as work,
+        tc.tile_pool(name="work", bufs=blocks) as work,
     ):
         offsets = lists.tile([P, n // PER_COLUMN], U16, name="offsets")
         nc.sync.dma_start(offsets[:], offs)
@@ -39,17 +39,16 @@ def tile_lookup_vg_addsig_out_kernel(tc, tab, y, offs, out):
 
         for b in range(blocks):
             block = slice(b * P, (b + 1) * P)
-            sums, opened = [], []
+            total = work.tile([P, n], F32, name="total")
+            openness = work.tile([P, n], F32, name="openness")
+            product = work.tile([P, n], F32, name="product")
             for p in range(pieces):
                 piece = slice(p * PIECE, (p + 1) * PIECE)
                 part = offsets[:, p * PIECE // PER_COLUMN : (p + 1) * PIECE // PER_COLUMN]
-                total = work.tile([P, PIECE], F32, name="total")
-                nc.vector.tensor_tensor(total[:], values[b][:].indirect(part), streams[b][:, piece], ADD)
-                sums.append(total)
-                openness = work.tile([P, PIECE], F32, name="openness")
-                nc.scalar.activation(openness[:], gates[b][:].indirect(part), SIGMOID)
-                opened.append(openness)
-            for p in range(pieces):
-                product = work.tile([P, PIECE], F32, name="product")
-                nc.vector.tensor_tensor(product[:], sums[p][:], opened[p][:], MULT)
-                nc.sync.dma_start(out[block, p * PIECE : (p + 1) * PIECE], product[:])
+                nc.vector.tensor_tensor(total[:, piece], values[b][:].indirect(part), streams[b][:, piece], ADD)
+                nc.scalar.activation(openness[:, piece], gates[b][:].indirect(part), SIGMOID)
+            width = n if b < blocks - 1 else PIECE
+            for start in range(0, n, width):
+                run = slice(start, start + width)
+                nc.vector.tensor_tensor(product[:, run], total[:, run], openness[:, run], MULT)
+                nc.sync.dma_start(out[block, run], product[:, run])

@@ -31,8 +31,11 @@ def tile_lookup_vg_addsig_out_kernel(tc, tab, y, offs, out):
             stream = loads.tile([P, n], F32, name="stream")
             gate = loads.tile([P, places], F32, name="gate")
             nc.sync.dma_start(value[:], tab[0, block, :])
-            nc.sync.dma_start(stream[:], y[block, :])
+            ahead = n if b < blocks - 1 else PIECE
+            nc.sync.dma_start(stream[:, :ahead], y[block, :ahead])
             nc.sync.dma_start(gate[:], tab[1, block, :])
+            if ahead < n:
+                nc.sync.dma_start(stream[:, ahead:], y[block, ahead:])
             values.append(value)
             streams.append(stream)
             gates.append(gate)

import concourse.mybir as mybir

F32, U16 = mybir.dt.float32, mybir.dt.uint16
ADD, MULT = mybir.AluOpType.add, mybir.AluOpType.mult
SIGMOID = mybir.ActivationFunctionType.Sigmoid

P = 128
PIECE = 512
PER_COLUMN = 16


def tile_lookup_vg_addsig_out_kernel(tc, tab, y, offs, out):
    nc = tc.nc
    rows, n = y.shape
    places = tab.shape[2]
    blocks = rows // P
    pieces = n // PIECE

    with (
        tc.tile_pool(name="lists", bufs=1) as lists,
        tc.tile_pool(name="loads", bufs=blocks) as loads,
        tc.tile_pool(name="work", bufs=blocks) as work,
    ):
        offsets = lists.tile([P, n // PER_COLUMN], U16, name="offsets")
        nc.sync.dma_start(offsets[:], offs)

        values, streams, gates = [], [], []
        for b in range(blocks):
            block = slice(b * P, (b + 1) * P)
            value = loads.tile([P, places], F32, name="value")
            stream = loads.tile([P, n], F32, name="stream")
            gate = loads.tile([P, places], F32, name="gate")
            nc.sync.dma_start(value[:], tab[0, block, :])
            ahead = n if b < blocks - 1 else PIECE
            nc.sync.dma_start(stream[:, :ahead], y[block, :ahead])
            nc.sync.dma_start(gate[:], tab[1, block, :])
            if ahead < n:
                nc.sync.dma_start(stream[:, ahead:], y[block, ahead:])
            values.append(value)
            streams.append(stream)
            gates.append(gate)

        for b in range(blocks):
            block = slice(b * P, (b + 1) * P)
            total = work.tile([P, n], F32, name="total")
            openness = work.tile([P, n], F32, name="openness")
            product = work.tile([P, n], F32, name="product")
            for p in range(pieces):
                piece = slice(p * PIECE, (p + 1) * PIECE)
                part = offsets[:, p * PIECE // PER_COLUMN : (p + 1) * PIECE // PER_COLUMN]
                nc.vector.tensor_tensor(total[:, piece], values[b][:].indirect(part), streams[b][:, piece], ADD)
                nc.scalar.activation(openness[:, piece], gates[b][:].indirect(part), SIGMOID)
            width = n if b < blocks - 1 else PIECE
            for start in range(0, n, width):
                run = slice(start, start + width)
                nc.vector.tensor_tensor(product[:, run], total[:, run], openness[:, run], MULT)
                nc.sync.dma_start(out[block, run], product[:, run])
